import numpy as np
import ml_dtypes


def mxq(x, axis, fmt="e4m3"):
    dtype, down = {"e4m3": (ml_dtypes.float8_e4m3fn, 7), "e5m2": (ml_dtypes.float8_e5m2, 14)}[fmt]
    v = np.moveaxis(np.asarray(x, np.float32).astype(ml_dtypes.bfloat16).astype(np.float64), axis, -1)
    blocks = v.reshape(v.shape[:-1] + (-1, 32))
    amax = np.abs(blocks).max(-1, keepdims=True)
    byte = np.maximum(np.where(amax > 0, np.frexp(amax)[1] - 1 + 127, 0) - down, 1)
    scale = np.exp2(byte - 127.0)
    codes = (blocks / scale).astype(np.float32).astype(dtype).astype(np.float64)
    return np.moveaxis((codes * scale).reshape(v.shape), -1, axis)


WIDE = False


def mx_kscale(k):
    if not WIDE:
        return np.ones(k)
    levels = np.array([10, -10, 5, -5, 0])
    if k % 512:
        return np.exp2(np.random.permutation(np.resize(levels, k // 32))).repeat(32)
    a = np.empty((k // 512, 16))
    for p in range(k // 512):
        a[p, :8] = np.random.permutation(np.resize(levels, 8))
        for g in range(8):
            far = levels[np.abs(levels - a[p, g]) >= 10]
            a[p, g + 8] = far[np.random.randint(len(far))]
    return np.exp2(a.ravel()).repeat(32)


def f64(x):
    return np.asarray(x).astype(np.float64)


def striped(idx):
    return np.tile(np.asarray(idx).reshape(-1, 16).T, (8, 1)).astype(np.uint16)


def unstriped(offs):
    return offs[:16].T.reshape(-1).astype(np.int64)


E2M1 = np.array([0.0, 0.5, 1.0, 1.5, 2.0, 3.0, 4.0, 6.0, -0.0, -0.5, -1.0, -1.5, -2.0, -3.0, -4.0, -6.0])


def pack_weight(w, fmt):
    k, n = w.shape
    w = f64(np.asarray(w, np.float32).astype(ml_dtypes.bfloat16)).reshape(k // 32, 32, n)
    amax = np.abs(w).max(1)
    if fmt == "e4m3":
        byte = np.frexp(amax)[1] - 1 + 127 - 7
    else:
        mant, ex = np.frexp(amax / 6.0)
        byte = np.where(mant > 0.5, ex, ex - 1) + 127
    byte = np.clip(np.where(amax > 0, byte, 1), 1, 254)
    scaled = (w * np.exp2(127.0 - byte)[:, None, :]).reshape(k, n).astype(np.float32)
    by_word = np.ascontiguousarray(scaled.reshape(k // 512, 128, 4, n).transpose(0, 1, 3, 2))
    if fmt == "e4m3":
        words = by_word.astype(ml_dtypes.float8_e4m3fn).view(np.uint8)
    else:
        c = by_word.astype(ml_dtypes.float4_e2m1fn).view(np.uint8) & 0xF
        words = (c[..., 0::2] | (c[..., 1::2] << 4)).reshape(k // 512, 128, 2 * n)
    return np.ascontiguousarray(words), np.ascontiguousarray(byte.astype(np.uint8).reshape(k // 512, 16, n))


def unpack_weight(words, scales, fmt):
    g, _, n = scales.shape
    words = np.ascontiguousarray(words).reshape(g, 128, n, -1)
    if fmt == "e4m3":
        vals = words.view(ml_dtypes.float8_e4m3fn).astype(np.float64)
    else:
        nib = np.empty((g, 128, n, 4), np.uint8)
        nib[..., 0::2] = words & 0xF
        nib[..., 1::2] = words >> 4
        vals = E2M1[nib]
    vals = vals * np.repeat(np.exp2(scales.astype(np.float64) - 127.0), 8, axis=1)[..., None]
    return vals.transpose(0, 1, 3, 2).reshape(g * 512, n)


def bf(x):
    return np.asarray(x, np.float32).astype(ml_dtypes.bfloat16)


def planes(Y):
    r, m = Y.shape
    b = f64(bf(Y)).reshape(r // 32, 32, m)
    amax = np.abs(b).max(1)
    byte = np.clip(np.where(amax > 0, np.frexp(amax)[1] - 1 + 127 - 7, 1), 1, 254)
    codes = (b * np.exp2(127.0 - byte)[:, None, :]).reshape(r, m).astype(np.float32).astype(ml_dtypes.float8_e4m3fn).view(np.uint8)
    words = codes.reshape(r // 512, 128, 4, m).transpose(0, 1, 3, 2)
    return np.ascontiguousarray(words), np.ascontiguousarray(byte.astype(np.uint8).reshape(r // 512, 16, m))


K, T, S, L, J, N = 512, 1024, 1024, 512, 512, 512


def setup_inputs():
    n = np.random.standard_normal
    idx = np.random.permutation(T)[:J]
    idx2 = np.random.permutation(S)[:J]
    fk = mx_kscale(K)
    fl = mx_kscale(L)
    wp = pack_weight(n((K, N)) * 1 / np.sqrt(K) * fk[:, None], "e4m3")
    xqp = pack_weight(n((L, S)) / fl[:, None], "e2m1")
    wqp = pack_weight(n((L, N)) * 1 / np.sqrt(L) * fl[:, None], "e4m3")
    return {
        "xa": (n((K, T))).astype(np.float32),
        "xb": (n((K, S))).astype(np.float32),
        "fk": (np.random.uniform(0.5, 2.0, (K, 1)) / fk[:, None]).astype(np.float32),
        "w_words": wp[0],
        "w_scales": wp[1],
        "xq_words": xqp[0],
        "xq_scales": xqp[1],
        "wq_words": wqp[0],
        "wq_scales": wqp[1],
        "offs": striped(idx),
        "offs2": striped(idx2),
    }


def reference(xa, xb, fk, w_words, w_scales, xq_words, xq_scales, wq_words, wq_scales, offs, offs2):
    idx = unstriped(offs)
    idx2 = unstriped(offs2)
    wu = unpack_weight(w_words, w_scales, "e4m3")
    xqu = unpack_weight(xq_words, xq_scales, "e2m1")
    wqu = unpack_weight(wq_words, wq_scales, "e4m3")
    pr = f64(xa)[:, idx] * f64(xb)[:, idx2] * f64(fk)
    prq = mxq(pr, 0, "e4m3")
    xqidx2g = xqu[:, idx2]
    y = wu.T @ prq + wqu.T @ xqidx2g
    words, scales = planes(y)
    return y, words, scales

@@ -1,0 +1,184 @@
+from contextlib import ExitStack
+
+import concourse.mybir as mybir
+
+K, T, S, L, J, N = 512, 1024, 1024, 512, 512, 512
+FLOPS = 2 * (K + L) * N * J
+
+F32 = mybir.dt.float32
+BF16 = mybir.dt.bfloat16
+I32 = mybir.dt.int32
+U32 = mybir.dt.uint32
+U16 = mybir.dt.uint16
+U8 = mybir.dt.uint8
+FP8X4 = mybir.dt.float8_e4m3fn_x4
+FP4X4 = mybir.dt.float4_e2m1fn_x4
+COPY = mybir.ActivationFunctionType.Copy
+MULT = mybir.AluOpType.mult
+
+P = 128
+PACK = 4
+QUADS = 4
+SLICE = 128
+SLICES = J // SLICE
+LIST_COLS = SLICE // 16
+W_ROW = 4
+
+
+def load_scale_rows(queue, plane, scales, row):
+    for q in range(QUADS):
+        queue.dma_start(
+            out=plane[32 * q + row : 32 * q + row + 4, :].bitcast(I32),
+            in_=scales[0, 4 * q : 4 * q + 4, :].bitcast(I32),
+        )
+
+
+def tile_list_products_of_two_tables_pl_kernel(
+    tc, xa, xb, fk, w_words, w_scales, xq_words, xq_scales, wq_words, wq_scales, offs, offs2, out_0, out_1, out_2
+):
+    nc = tc.nc
+    with ExitStack() as ctx:
+        lists = ctx.enter_context(tc.tile_pool(name="lists", bufs=1))
+        keep = ctx.enter_context(tc.tile_pool(name="keep", bufs=1))
+        psum = ctx.enter_context(tc.psum_pool(name="psum", bufs=1))
+
+        list_a = lists.tile([P, J // 16], U16, name="list_a")
+        list_b = lists.tile([P, J // 16], U16, name="list_b")
+
+        xq_scale_table = keep.tile([P, S], U8, name="xq_scale_table", align_bytes=64)
+        weight_scale_rows = keep.tile([P, N], U8, name="weight_scale_rows", align_bytes=64)
+        nc.vector.memset(xq_scale_table[:].bitcast(I32), 0)
+        nc.vector.memset(weight_scale_rows[:].bitcast(I32), 0)
+
+        xa_rows = xa.rearrange("(p t) c -> p t c", t=PACK)
+        xb_rows = xb.rearrange("(p t) c -> p t c", t=PACK)
+        xa_planes = [keep.tile([P, T], F32, name="xa_plane%d" % t) for t in range(PACK)]
+        xb_planes = [keep.tile([P, S], F32, name="xb_plane%d" % t) for t in range(PACK)]
+        xq_table = keep.tile([P, S], U16, name="xq_table", align_bytes=64)
+        factors = keep.tile([P, PACK], F32, name="factors")
+        w_loaded = keep.tile([P, N], I32, name="w_loaded", align_bytes=64)
+        wq_loaded = keep.tile([P, N], I32, name="wq_loaded", align_bytes=64)
+
+        nc.sync.dma_start(list_b[:], offs2)
+        nc.sync.dma_start(out=xq_table[:].bitcast(I32), in_=xq_words[0].bitcast(I32))
+        nc.sync.dma_start(list_a[:], offs)
+        nc.sync.dma_start(out=xa_planes[0][:], in_=xa_rows[:, 0, :])
+        nc.sync.dma_start(out=xa_planes[1][:], in_=xa_rows[:, 1, :])
+        nc.sync.dma_start(out=xb_planes[0][:], in_=xb_rows[:, 0, :])
+        nc.sync.dma_start(out=factors[:], in_=fk.rearrange("(p t) o -> p (t o)", t=PACK))
+        nc.sync.dma_start(out=xa_planes[2][:], in_=xa_rows[:, 2, :])
+        nc.sync.dma_start(out=xb_planes[1][:], in_=xb_rows[:, 1, :])
+        load_scale_rows(nc.sync, xq_scale_table, xq_scales, 0)
+        nc.sync.dma_start(out=xb_planes[2][:], in_=xb_rows[:, 2, :])
+        load_scale_rows(nc.sync, weight_scale_rows, wq_scales, 0)
+        load_scale_rows(nc.sync, weight_scale_rows, w_scales, W_ROW)
+        nc.sync.dma_start(out=wq_loaded[:], in_=wq_words[0].rearrange("p n t -> p (n t)").bitcast(I32))
+        nc.sync.dma_start(out=w_loaded[:], in_=w_words[0].rearrange("p n t -> p (n t)").bitcast(I32))
+        nc.sync.dma_start(out=xa_planes[3][:], in_=xa_rows[:, 3, :])
+        nc.sync.dma_start(out=xb_planes[3][:], in_=xb_rows[:, 3, :])
+
+        xq_picked = keep.tile([P, J], U16, name="xq_picked", align_bytes=64)
+        nc.vector.tensor_copy(xq_picked[:], xq_table[:].indirect(list_b[:]))
+
+        last = PACK - 1
+        pr_grouped = keep.tile([P, J, PACK], BF16, name="pr_grouped", align_bytes=64)
+        for t in range(last):
+            xa_picked = keep.tile([P, J], F32, name="xa_picked%d" % t)
+            products = keep.tile([P, J], F32, name="products%d" % t)
+            nc.vector.tensor_copy(xa_picked[:], xa_planes[t][:].indirect(list_a[:]))
+            nc.vector.tensor_tensor(products[:], xb_planes[t][:].indirect(list_b[:]), xa_picked[:], MULT)
+            nc.scalar.activation(pr_grouped[:, :, t], products[:], COPY, scale=factors[:, t : t + 1])
+
+        xq_picked_scales = keep.tile([P, J], U8, name="xq_picked_scales", align_bytes=64)
+        nc.vector.tensor_copy(xq_picked_scales[:], xq_scale_table[:].indirect(list_b[:]))
+
+        w_dealt = keep.tile([P, PACK, P], I32, name="w_dealt", align_bytes=64)
+        wq_dealt = keep.tile([P, PACK, P], I32, name="wq_dealt", align_bytes=64)
+        weight_scales = keep.tile([P, PACK, P], U8, name="weight_scales", align_bytes=64)
+        nc.vector.tensor_copy(
+            weight_scales[:].rearrange("p t m -> p m t"), weight_scale_rows[:].rearrange("p (m t) -> p m t", t=PACK)
+        )
+        for dealt, loaded in ((wq_dealt, wq_loaded), (w_dealt, w_loaded)):
+            nc.vector.tensor_copy(dealt[:].rearrange("p t m -> p m t"), loaded[:].rearrange("p (m t) -> p m t", t=PACK))
+
+        banks = [psum.tile([P, PACK, SLICE], F32, name="bank%d" % s) for s in range(SLICES)]
+        for s in range(SLICES):
+            cols = slice(s * SLICE, (s + 1) * SLICE)
+            for t in range(PACK):
+                nc.tensor.matmul_mx(
+                    out=banks[s][:, t, :],
+                    lhsT=wq_dealt[:, t, :].bitcast(FP8X4),
+                    lhsT_scale=weight_scales[:, t, :],
+                    rhs=xq_picked[:, cols].bitcast(FP4X4),
+                    rhs_scale=xq_picked_scales[:, cols],
+                    start=(t == 0),
+                    stop=False,
+                )
+
+        pr_scales = keep.tile([P, J], U8, name="pr_scales", align_bytes=64)
+        y_codes = keep.tile([P, J], U32, name="y_codes", align_bytes=64)
+        y_scales = keep.tile([P, J], U8, name="y_scales", align_bytes=64)
+        y_rows = out_0.rearrange("(p t) j -> p t j", t=PACK)
+        y_words = out_1[0].rearrange("p j t -> p (j t)").bitcast(I32)
+        xa_slices = {}
+
+        def pick_xa(s):
+            xa_slices[s] = keep.tile([P, SLICE], F32, name="xa_slice%d" % s, tag="xa_slice", bufs=2)
+            picks = list_a[:, s * LIST_COLS : (s + 1) * LIST_COLS]
+            nc.vector.tensor_copy(xa_slices[s][:], xa_planes[last][:].indirect(picks))
+
+        def finish_pr(s):
+            cols = slice(s * SLICE, (s + 1) * SLICE)
+            picks = list_b[:, s * LIST_COLS : (s + 1) * LIST_COLS]
+            if s < SLICES - 1:
+                product = keep.tile([P, SLICE], F32, name="product%d" % s, tag="product", bufs=2)
+            else:
+                product = keep.tile([P, SLICE], F32, name="product%d" % s, tag="pr_codes0", align_bytes=64)
+            nc.vector.tensor_tensor(product[:], xb_planes[last][:].indirect(picks), xa_slices[s][:], MULT)
+            nc.scalar.activation(pr_grouped[:, cols, last], product[:], COPY, scale=factors[:, last : last + 1])
+
+        def multiply(s):
+            cols = slice(s * SLICE, (s + 1) * SLICE)
+            pr_codes = keep.tile([P, SLICE], U32, name="pr_codes%d" % s, align_bytes=64)
+            nc.vector.quantize_mx(
+                out=pr_codes[:].bitcast(FP8X4),
+                scales=pr_scales[:, cols],
+                in_=pr_grouped[:, cols, :].rearrange("p j t -> p (j t)"),
+            )
+            for t in range(PACK):
+                nc.tensor.matmul_mx(
+                    out=banks[s][:, t, :],
+                    lhsT=w_dealt[:, t, :].bitcast(FP8X4),
+                    lhsT_scale=weight_scales[W_ROW:P, t, :],
+                    rhs=pr_codes[:].bitcast(FP8X4),
+                    rhs_scale=pr_scales[:, cols],
+                    start=False,
+                    stop=(t == PACK - 1),
+                )
+
+        def hand_out(s):
+            cols = slice(s * SLICE, (s + 1) * SLICE)
+            y = keep.tile([P, PACK, SLICE], F32, name="y%d" % s)
+            nc.scalar.copy(y[:], banks[s][:])
+            nc.sync.dma_start(out=y_rows[:, :, cols], in_=y[:])
+            y_grouped = keep.tile([P, SLICE, PACK], BF16, name="y_grouped%d" % s, align_bytes=64)
+            nc.vector.tensor_copy(
+                y_grouped[:].rearrange("p (c i) t -> p c t i", i=4), y[:].rearrange("p t (c i) -> p c t i", i=4)
+            )
+            nc.vector.quantize_mx(
+                out=y_codes[:, cols].bitcast(FP8X4),
+                scales=y_scales[:, cols],
+                in_=y_grouped[:].rearrange("p j t -> p (j t)"),
+            )
+            nc.sync.dma_start(out=y_words[:, cols], in_=y_codes[:, cols].bitcast(I32))
+
+        stages = (pick_xa, finish_pr, multiply, hand_out)
+        for step in range(SLICES + len(stages) - 1):
+            for depth in reversed(range(len(stages))):
+                if 0 <= step - depth < SLICES:
+                    stages[depth](step - depth)
+        for q in range(QUADS):
+            queue = nc.sync if q % 2 == 0 else nc.scalar
+            queue.dma_start(
+                out=out_2[0, 4 * q : 4 * q + 4, :].bitcast(I32), in_=y_scales[32 * q : 32 * q + 4, :].bitcast(I32)
+            )

@@ -25,8 +25,8 @@ LIST_COLS = SLICE // 16
 W_ROW = 4
 
 
-def load_scale_rows(queue, plane, scales, row):
-    for q in range(QUADS):
+def load_scale_rows(queue, plane, scales, row, quads):
+    for q in quads:
         queue.dma_start(
             out=plane[32 * q + row : 32 * q + row + 4, :].bitcast(I32),
             in_=scales[0, 4 * q : 4 * q + 4, :].bitcast(I32),
@@ -64,17 +64,17 @@ def tile_list_products_of_two_tables_pl_kernel(
         nc.sync.dma_start(list_a[:], offs)
         nc.sync.dma_start(out=xa_planes[0][:], in_=xa_rows[:, 0, :])
         nc.sync.dma_start(out=xa_planes[1][:], in_=xa_rows[:, 1, :])
-        nc.sync.dma_start(out=xb_planes[0][:], in_=xb_rows[:, 0, :])
         nc.sync.dma_start(out=factors[:], in_=fk.rearrange("(p t) o -> p (t o)", t=PACK))
+        nc.sync.dma_start(out=xb_planes[0][:], in_=xb_rows[:, 0, :])
         nc.sync.dma_start(out=xa_planes[2][:], in_=xa_rows[:, 2, :])
         nc.sync.dma_start(out=xb_planes[1][:], in_=xb_rows[:, 1, :])
-        load_scale_rows(nc.sync, xq_scale_table, xq_scales, 0)
         nc.sync.dma_start(out=xb_planes[2][:], in_=xb_rows[:, 2, :])
-        load_scale_rows(nc.sync, weight_scale_rows, wq_scales, 0)
-        load_scale_rows(nc.sync, weight_scale_rows, w_scales, W_ROW)
+        load_scale_rows(nc.sync, xq_scale_table, xq_scales, 0, range(QUADS))
         nc.sync.dma_start(out=wq_loaded[:], in_=wq_words[0].rearrange("p n t -> p (n t)").bitcast(I32))
         nc.sync.dma_start(out=w_loaded[:], in_=w_words[0].rearrange("p n t -> p (n t)").bitcast(I32))
+        load_scale_rows(nc.sync, weight_scale_rows, wq_scales, 0, range(QUADS))
         nc.sync.dma_start(out=xa_planes[3][:], in_=xa_rows[:, 3, :])
+        load_scale_rows(nc.sync, weight_scale_rows, w_scales, W_ROW, range(QUADS))
         nc.sync.dma_start(out=xb_planes[3][:], in_=xb_rows[:, 3, :])
 
         xq_picked = keep.tile([P, J], U16, name="xq_picked", align_bytes=64)
@@ -101,19 +101,24 @@ def tile_list_products_of_two_tables_pl_kernel(
         for dealt, loaded in ((wq_dealt, wq_loaded), (w_dealt, w_loaded)):
             nc.vector.tensor_copy(dealt[:].rearrange("p t m -> p m t"), loaded[:].rearrange("p (m t) -> p m t", t=PACK))
 
-        banks = [psum.tile([P, PACK, SLICE], F32, name="bank%d" % s) for s in range(SLICES)]
+        groups = [[(0, PACK)]] * (SLICES - 1) + [[(0, PACK // 2), (PACK // 2, PACK)]]
+        banks = [
+            [psum.tile([P, PACK, SLICE], F32, name="bank%d_%d" % (s, first)) for first, end in groups[s]]
+            for s in range(SLICES)
+        ]
         for s in range(SLICES):
             cols = slice(s * SLICE, (s + 1) * SLICE)
-            for t in range(PACK):
-                nc.tensor.matmul_mx(
-                    out=banks[s][:, t, :],
-                    lhsT=wq_dealt[:, t, :].bitcast(FP8X4),
-                    lhsT_scale=weight_scales[:, t, :],
-                    rhs=xq_picked[:, cols].bitcast(FP4X4),
-                    rhs_scale=xq_picked_scales[:, cols],
-                    start=(t == 0),
-                    stop=False,
-                )
+            for bank, (first, end) in zip(banks[s], groups[s]):
+                for t in range(first, end):
+                    nc.tensor.matmul_mx(
+                        out=bank[:, t, :],
+                        lhsT=wq_dealt[:, t, :].bitcast(FP8X4),
+                        lhsT_scale=weight_scales[:, t, :],
+                        rhs=xq_picked[:, cols].bitcast(FP4X4),
+                        rhs_scale=xq_picked_scales[:, cols],
+                        start=(t == first),
+                        stop=False,
+                    )
 
         pr_scales = keep.tile([P, J], U8, name="pr_scales", align_bytes=64)
         y_codes = keep.tile([P, J], U32, name="y_codes", align_bytes=64)
@@ -121,6 +126,7 @@ def tile_list_products_of_two_tables_pl_kernel(
         y_rows = out_0.rearrange("(p t) j -> p t j", t=PACK)
         y_words = out_1[0].rearrange("p j t -> p (j t)").bitcast(I32)
         xa_slices = {}
+        y_slices = {}
 
         def pick_xa(s):
             xa_slices[s] = keep.tile([P, SLICE], F32, name="xa_slice%d" % s, tag="xa_slice", bufs=2)
@@ -145,22 +151,29 @@ def tile_list_products_of_two_tables_pl_kernel(
                 scales=pr_scales[:, cols],
                 in_=pr_grouped[:, cols, :].rearrange("p j t -> p (j t)"),
             )
-            for t in range(PACK):
-                nc.tensor.matmul_mx(
-                    out=banks[s][:, t, :],
-                    lhsT=w_dealt[:, t, :].bitcast(FP8X4),
-                    lhsT_scale=weight_scales[W_ROW:P, t, :],
-                    rhs=pr_codes[:].bitcast(FP8X4),
-                    rhs_scale=pr_scales[:, cols],
-                    start=False,
-                    stop=(t == PACK - 1),
-                )
+            for bank, (first, end) in zip(banks[s], groups[s]):
+                for t in range(first, end):
+                    nc.tensor.matmul_mx(
+                        out=bank[:, t, :],
+                        lhsT=w_dealt[:, t, :].bitcast(FP8X4),
+                        lhsT_scale=weight_scales[W_ROW:P, t, :],
+                        rhs=pr_codes[:].bitcast(FP8X4),
+                        rhs_scale=pr_scales[:, cols],
+                        start=False,
+                        stop=(t == end - 1),
+                    )
 
         def hand_out(s):
             cols = slice(s * SLICE, (s + 1) * SLICE)
             y = keep.tile([P, PACK, SLICE], F32, name="y%d" % s)
-            nc.scalar.copy(y[:], banks[s][:])
+            y_slices[s] = y
+            for bank, (first, end) in zip(banks[s], groups[s]):
+                nc.scalar.copy(y[:, first:end, :], bank[:, first:end, :])
             nc.sync.dma_start(out=y_rows[:, :, cols], in_=y[:])
+
+        def make_planes(s):
+            cols = slice(s * SLICE, (s + 1) * SLICE)
+            y = y_slices[s]
             y_grouped = keep.tile([P, SLICE, PACK], BF16, name="y_grouped%d" % s, align_bytes=64)
             nc.vector.tensor_copy(
                 y_grouped[:].rearrange("p (c i) t -> p c t i", i=4), y[:].rearrange("p t (c i) -> p c t i", i=4)
@@ -170,13 +183,15 @@ def tile_list_products_of_two_tables_pl_kernel(
                 scales=y_scales[:, cols],
                 in_=y_grouped[:].rearrange("p j t -> p (j t)"),
             )
-            nc.sync.dma_start(out=y_words[:, cols], in_=y_codes[:, cols].bitcast(I32))
+            if s >= SLICES - 2:
+                done = slice(0 if s == SLICES - 2 else s * SLICE, (s + 1) * SLICE)
+                nc.sync.dma_start(out=y_words[:, done], in_=y_codes[:, done].bitcast(I32))
 
-        stages = (pick_xa, finish_pr, multiply, hand_out)
-        for step in range(SLICES + len(stages) - 1):
-            for depth in reversed(range(len(stages))):
-                if 0 <= step - depth < SLICES:
-                    stages[depth](step - depth)
+        stages = ((finish_pr, 1), (multiply, 2), (pick_xa, 0), (hand_out, 3), (make_planes, 5))
+        for step in range(SLICES + 5):
+            for stage, delay in stages:
+                if 0 <= step - delay < SLICES:
+                    stage(step - delay)
         for q in range(QUADS):
             queue = nc.sync if q % 2 == 0 else nc.scalar
             queue.dma_start(

@@ -63,11 +63,11 @@ def tile_list_products_of_two_tables_pl_kernel(
         nc.sync.dma_start(out=xq_table[:].bitcast(I32), in_=xq_words[0].bitcast(I32))
         nc.sync.dma_start(list_a[:], offs)
         nc.sync.dma_start(out=xa_planes[0][:], in_=xa_rows[:, 0, :])
-        nc.sync.dma_start(out=xa_planes[1][:], in_=xa_rows[:, 1, :])
-        nc.sync.dma_start(out=factors[:], in_=fk.rearrange("(p t) o -> p (t o)", t=PACK))
         nc.sync.dma_start(out=xb_planes[0][:], in_=xb_rows[:, 0, :])
-        nc.sync.dma_start(out=xa_planes[2][:], in_=xa_rows[:, 2, :])
+        nc.sync.dma_start(out=factors[:], in_=fk.rearrange("(p t) o -> p (t o)", t=PACK))
+        nc.sync.dma_start(out=xa_planes[1][:], in_=xa_rows[:, 1, :])
         nc.sync.dma_start(out=xb_planes[1][:], in_=xb_rows[:, 1, :])
+        nc.sync.dma_start(out=xa_planes[2][:], in_=xa_rows[:, 2, :])
         nc.sync.dma_start(out=xb_planes[2][:], in_=xb_rows[:, 2, :])
         load_scale_rows(nc.sync, xq_scale_table, xq_scales, 0, range(QUADS))
         nc.sync.dma_start(out=wq_loaded[:], in_=wq_words[0].rearrange("p n t -> p (n t)").bitcast(I32))
@@ -86,7 +86,9 @@ def tile_list_products_of_two_tables_pl_kernel(
             xa_picked = keep.tile([P, J], F32, name="xa_picked%d" % t)
             products = keep.tile([P, J], F32, name="products%d" % t)
             nc.vector.tensor_copy(xa_picked[:], xa_planes[t][:].indirect(list_a[:]))
-            nc.vector.tensor_tensor(products[:], xb_planes[t][:].indirect(list_b[:]), xa_picked[:], MULT)
+            xb_picked = keep.tile([P, J], F32, name="xb_picked%d" % t)
+            nc.vector.tensor_copy(xb_picked[:], xb_planes[t][:].indirect(list_b[:]))
+            nc.gpsimd.tensor_tensor(products[:], xa_picked[:], xb_picked[:], MULT)
             nc.scalar.activation(pr_grouped[:, :, t], products[:], COPY, scale=factors[:, t : t + 1])
 
         xq_picked_scales = keep.tile([P, J], U8, name="xq_picked_scales", align_bytes=64)
@@ -96,10 +98,14 @@ def tile_list_products_of_two_tables_pl_kernel(
         wq_dealt = keep.tile([P, PACK, P], I32, name="wq_dealt", align_bytes=64)
         weight_scales = keep.tile([P, PACK, P], U8, name="weight_scales", align_bytes=64)
         nc.vector.tensor_copy(
-            weight_scales[:].rearrange("p t m -> p m t"), weight_scale_rows[:].rearrange("p (m t) -> p m t", t=PACK)
+            weight_scales[:].rearrange("p t (c i) -> p c t i", i=16),
+            weight_scale_rows[:].rearrange("p (c i t) -> p c t i", i=16, t=PACK),
         )
         for dealt, loaded in ((wq_dealt, wq_loaded), (w_dealt, w_loaded)):
-            nc.vector.tensor_copy(dealt[:].rearrange("p t m -> p m t"), loaded[:].rearrange("p (m t) -> p m t", t=PACK))
+            nc.vector.tensor_copy(
+                dealt[:].rearrange("p t (c i) -> p c t i", i=4),
+                loaded[:].rearrange("p (c i t) -> p c t i", i=4, t=PACK),
+            )
 
         groups = [[(0, PACK)]] * (SLICES - 1) + [[(0, PACK // 2), (PACK // 2, PACK)]]
         banks = [

@@ -18,19 +18,31 @@ MULT = mybir.AluOpType.mult
 
 P = 128
 PACK = 4
-QUADS = 4
+QUADRANT = 32
+SCALE_ROWS = 4
+QUADRANTS = P // QUADRANT
+LIST_GROUP = 16
+LINE = 16
 SLICE = 128
 SLICES = J // SLICE
-LIST_COLS = SLICE // 16
-W_ROW = 4
+LIST_COLS = SLICE // LIST_GROUP
+W_ROW = SCALE_ROWS
+EARLY = 2
 
 
-def load_scale_rows(queue, plane, scales, row, quads):
-    for q in quads:
-        queue.dma_start(
-            out=plane[32 * q + row : 32 * q + row + 4, :].bitcast(I32),
-            in_=scales[0, 4 * q : 4 * q + 4, :].bitcast(I32),
+def load_scale_rows(nc, tile, scales, row, quadrants):
+    for q in quadrants:
+        nc.sync.dma_start(
+            out=tile[QUADRANT * q + row : QUADRANT * q + row + SCALE_ROWS, :].bitcast(I32),
+            in_=scales[0, SCALE_ROWS * q : SCALE_ROWS * (q + 1), :].bitcast(I32),
         )
+
+
+def deal_columns(nc, dealt, loaded, per_line):
+    nc.vector.tensor_copy(
+        dealt[:].rearrange("p t (c i) -> p c t i", i=per_line),
+        loaded[:].rearrange("p (c i t) -> p c t i", i=per_line, t=PACK),
+    )
 
 
 def tile_list_products_of_two_tables_pl_kernel(
@@ -42,8 +54,8 @@ def tile_list_products_of_two_tables_pl_kernel(
         keep = ctx.enter_context(tc.tile_pool(name="keep", bufs=1))
         psum = ctx.enter_context(tc.psum_pool(name="psum", bufs=1))
 
-        list_a = lists.tile([P, J // 16], U16, name="list_a")
-        list_b = lists.tile([P, J // 16], U16, name="list_b")
+        list_a = lists.tile([P, J // LIST_GROUP], U16, name="list_a")
+        list_b = lists.tile([P, J // LIST_GROUP], U16, name="list_b")
 
         xq_scale_table = keep.tile([P, S], U8, name="xq_scale_table", align_bytes=64)
         weight_scale_rows = keep.tile([P, N], U8, name="weight_scale_rows", align_bytes=64)
@@ -59,23 +71,29 @@ def tile_list_products_of_two_tables_pl_kernel(
         w_loaded = keep.tile([P, N], I32, name="w_loaded", align_bytes=64)
         wq_loaded = keep.tile([P, N], I32, name="wq_loaded", align_bytes=64)
 
+        def load_plane(planes, rows, t):
+            nc.sync.dma_start(out=planes[t][:], in_=rows[:, t, :])
+
+        low, high = range(QUADRANTS // 2), range(QUADRANTS // 2, QUADRANTS)
         nc.sync.dma_start(list_b[:], offs2)
         nc.sync.dma_start(out=xq_table[:].bitcast(I32), in_=xq_words[0].bitcast(I32))
         nc.sync.dma_start(list_a[:], offs)
-        nc.sync.dma_start(out=xa_planes[0][:], in_=xa_rows[:, 0, :])
-        nc.sync.dma_start(out=xb_planes[0][:], in_=xb_rows[:, 0, :])
+        load_plane(xa_planes, xa_rows, 0)
+        load_plane(xa_planes, xa_rows, 1)
+        load_scale_rows(nc, xq_scale_table, xq_scales, 0, low)
         nc.sync.dma_start(out=factors[:], in_=fk.rearrange("(p t) o -> p (t o)", t=PACK))
-        nc.sync.dma_start(out=xa_planes[1][:], in_=xa_rows[:, 1, :])
-        nc.sync.dma_start(out=xb_planes[1][:], in_=xb_rows[:, 1, :])
-        nc.sync.dma_start(out=xa_planes[2][:], in_=xa_rows[:, 2, :])
-        nc.sync.dma_start(out=xb_planes[2][:], in_=xb_rows[:, 2, :])
-        load_scale_rows(nc.sync, xq_scale_table, xq_scales, 0, range(QUADS))
+        load_plane(xb_planes, xb_rows, 0)
+        load_scale_rows(nc, xq_scale_table, xq_scales, 0, high)
+        load_plane(xa_planes, xa_rows, 2)
+        load_scale_rows(nc, weight_scale_rows, wq_scales, 0, low)
+        load_plane(xb_planes, xb_rows, 1)
+        load_scale_rows(nc, weight_scale_rows, wq_scales, 0, high)
+        load_plane(xb_planes, xb_rows, 2)
+        load_scale_rows(nc, weight_scale_rows, w_scales, W_ROW, range(QUADRANTS))
         nc.sync.dma_start(out=wq_loaded[:], in_=wq_words[0].rearrange("p n t -> p (n t)").bitcast(I32))
+        load_plane(xa_planes, xa_rows, 3)
+        load_plane(xb_planes, xb_rows, 3)
         nc.sync.dma_start(out=w_loaded[:], in_=w_words[0].rearrange("p n t -> p (n t)").bitcast(I32))
-        load_scale_rows(nc.sync, weight_scale_rows, wq_scales, 0, range(QUADS))
-        nc.sync.dma_start(out=xa_planes[3][:], in_=xa_rows[:, 3, :])
-        load_scale_rows(nc.sync, weight_scale_rows, w_scales, W_ROW, range(QUADS))
-        nc.sync.dma_start(out=xb_planes[3][:], in_=xb_rows[:, 3, :])
 
         xq_picked = keep.tile([P, J], U16, name="xq_picked", align_bytes=64)
         nc.vector.tensor_copy(xq_picked[:], xq_table[:].indirect(list_b[:]))
@@ -86,45 +104,41 @@ def tile_list_products_of_two_tables_pl_kernel(
             xa_picked = keep.tile([P, J], F32, name="xa_picked%d" % t)
             products = keep.tile([P, J], F32, name="products%d" % t)
             nc.vector.tensor_copy(xa_picked[:], xa_planes[t][:].indirect(list_a[:]))
-            xb_picked = keep.tile([P, J], F32, name="xb_picked%d" % t)
-            nc.vector.tensor_copy(xb_picked[:], xb_planes[t][:].indirect(list_b[:]))
-            nc.gpsimd.tensor_tensor(products[:], xa_picked[:], xb_picked[:], MULT)
+            nc.vector.tensor_tensor(products[:], xb_planes[t][:].indirect(list_b[:]), xa_picked[:], MULT)
             nc.scalar.activation(pr_grouped[:, :, t], products[:], COPY, scale=factors[:, t : t + 1])
 
-        xq_picked_scales = keep.tile([P, J], U8, name="xq_picked_scales", align_bytes=64)
-        nc.vector.tensor_copy(xq_picked_scales[:], xq_scale_table[:].indirect(list_b[:]))
+        early_scales = keep.tile([P, EARLY * SLICE], U8, name="early_scales", align_bytes=64)
+        nc.vector.tensor_copy(early_scales[:], xq_scale_table[:].indirect(list_b[:, : EARLY * LIST_COLS]))
 
         w_dealt = keep.tile([P, PACK, P], I32, name="w_dealt", align_bytes=64)
         wq_dealt = keep.tile([P, PACK, P], I32, name="wq_dealt", align_bytes=64)
         weight_scales = keep.tile([P, PACK, P], U8, name="weight_scales", align_bytes=64)
-        nc.vector.tensor_copy(
-            weight_scales[:].rearrange("p t (c i) -> p c t i", i=16),
-            weight_scale_rows[:].rearrange("p (c i t) -> p c t i", i=16, t=PACK),
-        )
-        for dealt, loaded in ((wq_dealt, wq_loaded), (w_dealt, w_loaded)):
-            nc.vector.tensor_copy(
-                dealt[:].rearrange("p t (c i) -> p c t i", i=4),
-                loaded[:].rearrange("p (c i t) -> p c t i", i=4, t=PACK),
-            )
+        deal_columns(nc, weight_scales, weight_scale_rows, LINE)
+        deal_columns(nc, wq_dealt, wq_loaded, LINE // 4)
+        deal_columns(nc, w_dealt, w_loaded, LINE // 4)
 
-        groups = [[(0, PACK)]] * (SLICES - 1) + [[(0, PACK // 2), (PACK // 2, PACK)]]
+        run_ranges = [[(0, PACK)]] * (SLICES - 1) + [[(0, PACK // 2), (PACK // 2, PACK)]]
         banks = [
-            [psum.tile([P, PACK, SLICE], F32, name="bank%d_%d" % (s, first)) for first, end in groups[s]]
+            [psum.tile([P, PACK, SLICE], F32, name="bank%d_%d" % (s, first)) for first, end in run_ranges[s]]
             for s in range(SLICES)
         ]
-        for s in range(SLICES):
+
+        def multiply_xq(s, picked_scales):
             cols = slice(s * SLICE, (s + 1) * SLICE)
-            for bank, (first, end) in zip(banks[s], groups[s]):
+            for bank, (first, end) in zip(banks[s], run_ranges[s]):
                 for t in range(first, end):
                     nc.tensor.matmul_mx(
                         out=bank[:, t, :],
                         lhsT=wq_dealt[:, t, :].bitcast(FP8X4),
                         lhsT_scale=weight_scales[:, t, :],
                         rhs=xq_picked[:, cols].bitcast(FP4X4),
-                        rhs_scale=xq_picked_scales[:, cols],
+                        rhs_scale=picked_scales,
                         start=(t == first),
                         stop=False,
                     )
+
+        for s in range(EARLY):
+            multiply_xq(s, early_scales[:, s * SLICE : (s + 1) * SLICE])
 
         pr_scales = keep.tile([P, J], U8, name="pr_scales", align_bytes=64)
         y_codes = keep.tile([P, J], U32, name="y_codes", align_bytes=64)
@@ -135,7 +149,7 @@ def tile_list_products_of_two_tables_pl_kernel(
         y_slices = {}
 
         def pick_xa(s):
-            xa_slices[s] = keep.tile([P, SLICE], F32, name="xa_slice%d" % s, tag="xa_slice", bufs=2)
+            xa_slices[s] = keep.tile([P, SLICE], F32, name="xa_slice%d" % s, tag="xa_slice%d" % (s % 2), align_bytes=64)
             picks = list_a[:, s * LIST_COLS : (s + 1) * LIST_COLS]
             nc.vector.tensor_copy(xa_slices[s][:], xa_planes[last][:].indirect(picks))
 
@@ -145,11 +159,17 @@ def tile_list_products_of_two_tables_pl_kernel(
             if s < SLICES - 1:
                 product = keep.tile([P, SLICE], F32, name="product%d" % s, tag="product", bufs=2)
             else:
-                product = keep.tile([P, SLICE], F32, name="product%d" % s, tag="pr_codes0", align_bytes=64)
+                product = keep.tile([P, SLICE], F32, name="product%d" % s, tag="pr_codes1", align_bytes=64)
             nc.vector.tensor_tensor(product[:], xb_planes[last][:].indirect(picks), xa_slices[s][:], MULT)
             nc.scalar.activation(pr_grouped[:, cols, last], product[:], COPY, scale=factors[:, last : last + 1])
+            if s >= EARLY:
+                late_scales = keep.tile(
+                    [P, SLICE], U8, name="late_scales%d" % s, tag="xa_slice%d" % (s % 2), align_bytes=64
+                )
+                nc.vector.tensor_copy(late_scales[:], xq_scale_table[:].indirect(picks))
+                multiply_xq(s, late_scales[:])
 
-        def multiply(s):
+        def multiply_pr(s):
             cols = slice(s * SLICE, (s + 1) * SLICE)
             pr_codes = keep.tile([P, SLICE], U32, name="pr_codes%d" % s, align_bytes=64)
             nc.vector.quantize_mx(
@@ -157,7 +177,7 @@ def tile_list_products_of_two_tables_pl_kernel(
                 scales=pr_scales[:, cols],
                 in_=pr_grouped[:, cols, :].rearrange("p j t -> p (j t)"),
             )
-            for bank, (first, end) in zip(banks[s], groups[s]):
+            for bank, (first, end) in zip(banks[s], run_ranges[s]):
                 for t in range(first, end):
                     nc.tensor.matmul_mx(
                         out=bank[:, t, :],
@@ -169,37 +189,54 @@ def tile_list_products_of_two_tables_pl_kernel(
                         stop=(t == end - 1),
                     )
 
-        def hand_out(s):
+        def store_y(s):
             cols = slice(s * SLICE, (s + 1) * SLICE)
-            y = keep.tile([P, PACK, SLICE], F32, name="y%d" % s)
-            y_slices[s] = y
-            for bank, (first, end) in zip(banks[s], groups[s]):
-                nc.scalar.copy(y[:, first:end, :], bank[:, first:end, :])
-            nc.sync.dma_start(out=y_rows[:, :, cols], in_=y[:])
+            y_slices[s] = keep.tile([P, PACK, SLICE], F32, name="y%d" % s)
+            for bank, (first, end) in zip(banks[s], run_ranges[s]):
+                nc.scalar.copy(y_slices[s][:, first:end, :], bank[:, first:end, :])
+            nc.sync.dma_start(out=y_rows[:, :, cols], in_=y_slices[s][:])
 
-        def make_planes(s):
-            cols = slice(s * SLICE, (s + 1) * SLICE)
-            y = y_slices[s]
-            y_grouped = keep.tile([P, SLICE, PACK], BF16, name="y_grouped%d" % s, align_bytes=64)
+        y_grouped = keep.tile([P, J, PACK], BF16, name="y_grouped", align_bytes=64)
+
+        def round_y(first, end):
+            s = first // SLICE
             nc.vector.tensor_copy(
-                y_grouped[:].rearrange("p (c i) t -> p c t i", i=4), y[:].rearrange("p t (c i) -> p c t i", i=4)
+                y_grouped[:, first:end, :].rearrange("p (c i) t -> p c t i", i=LINE // 4),
+                y_slices[s][:, :, first - s * SLICE : end - s * SLICE].rearrange("p t (c i) -> p c t i", i=LINE // 4),
             )
-            nc.vector.quantize_mx(
-                out=y_codes[:, cols].bitcast(FP8X4),
-                scales=y_scales[:, cols],
-                in_=y_grouped[:].rearrange("p j t -> p (j t)"),
-            )
-            if s >= SLICES - 2:
-                done = slice(0 if s == SLICES - 2 else s * SLICE, (s + 1) * SLICE)
-                nc.sync.dma_start(out=y_words[:, done], in_=y_codes[:, done].bitcast(I32))
 
-        stages = ((finish_pr, 1), (multiply, 2), (pick_xa, 0), (hand_out, 3), (make_planes, 5))
-        for step in range(SLICES + 5):
+        def quantize_y(first, end):
+            nc.vector.quantize_mx(
+                out=y_codes[:, first:end].bitcast(FP8X4),
+                scales=y_scales[:, first:end],
+                in_=y_grouped[:, first:end, :].rearrange("p j t -> p (j t)"),
+            )
+
+        stages = ((store_y, 3), (finish_pr, 1), (multiply_pr, 2), (pick_xa, 0))
+        steps = SLICES + max(delay for stage, delay in stages)
+        for step in range(steps):
             for stage, delay in stages:
                 if 0 <= step - delay < SLICES:
                     stage(step - delay)
-        for q in range(QUADS):
+            if step == steps - 2:
+                nc.scalar.copy(y_grouped[:, :SLICE, :], banks[0][0][:].rearrange("p t j -> p j t"))
+
+        tail = J - SLICE
+        round_y(SLICE, 2 * SLICE)
+        round_y(2 * SLICE, tail)
+        quantize_y(0, 2 * SLICE)
+        quantize_y(2 * SLICE, tail)
+        nc.sync.dma_start(out=y_words[:, :tail], in_=y_codes[:, :tail].bitcast(I32))
+        halves = ((tail, tail + SLICE // 2), (tail + SLICE // 2, J))
+        for first, end in halves:
+            round_y(first, end)
+        for first, end in halves:
+            quantize_y(first, end)
+        nc.sync.dma_start(out=y_words[:, tail:], in_=y_codes[:, tail:].bitcast(I32))
+
+        for q in range(QUADRANTS):
             queue = nc.sync if q % 2 == 0 else nc.scalar
             queue.dma_start(
-                out=out_2[0, 4 * q : 4 * q + 4, :].bitcast(I32), in_=y_scales[32 * q : 32 * q + 4, :].bitcast(I32)
+                out=out_2[0, SCALE_ROWS * q : SCALE_ROWS * (q + 1), :].bitcast(I32),
+                in_=y_scales[QUADRANT * q : QUADRANT * q + SCALE_ROWS, :].bitcast(I32),
             )

from contextlib import ExitStack

import concourse.mybir as mybir

K, T, S, L, J, N = 512, 1024, 1024, 512, 512, 512
FLOPS = 2 * (K + L) * N * J

F32 = mybir.dt.float32
BF16 = mybir.dt.bfloat16
I32 = mybir.dt.int32
U32 = mybir.dt.uint32
U16 = mybir.dt.uint16
U8 = mybir.dt.uint8
FP8X4 = mybir.dt.float8_e4m3fn_x4
FP4X4 = mybir.dt.float4_e2m1fn_x4
COPY = mybir.ActivationFunctionType.Copy
MULT = mybir.AluOpType.mult

P = 128
PACK = 4
QUADRANT = 32
SCALE_ROWS = 4
QUADRANTS = P // QUADRANT
LIST_GROUP = 16
LINE = 16
SLICE = 128
SLICES = J // SLICE
LIST_COLS = SLICE // LIST_GROUP
W_ROW = SCALE_ROWS
EARLY = 2


def load_scale_rows(nc, tile, scales, row, quadrants):
    for q in quadrants:
        nc.sync.dma_start(
            out=tile[QUADRANT * q + row : QUADRANT * q + row + SCALE_ROWS, :].bitcast(I32),
            in_=scales[0, SCALE_ROWS * q : SCALE_ROWS * (q + 1), :].bitcast(I32),
        )


def deal_columns(nc, dealt, loaded, per_line):
    nc.vector.tensor_copy(
        dealt[:].rearrange("p t (c i) -> p c t i", i=per_line),
        loaded[:].rearrange("p (c i t) -> p c t i", i=per_line, t=PACK),
    )


def tile_list_products_of_two_tables_pl_kernel(
    tc, xa, xb, fk, w_words, w_scales, xq_words, xq_scales, wq_words, wq_scales, offs, offs2, out_0, out_1, out_2
):
    nc = tc.nc
    with ExitStack() as ctx:
        lists = ctx.enter_context(tc.tile_pool(name="lists", bufs=1))
        keep = ctx.enter_context(tc.tile_pool(name="keep", bufs=1))
        psum = ctx.enter_context(tc.psum_pool(name="psum", bufs=1))

        list_a = lists.tile([P, J // LIST_GROUP], U16, name="list_a")
        list_b = lists.tile([P, J // LIST_GROUP], U16, name="list_b")

        xq_scale_table = keep.tile([P, S], U8, name="xq_scale_table", align_bytes=64)
        weight_scale_rows = keep.tile([P, N], U8, name="weight_scale_rows", align_bytes=64)
        nc.vector.memset(xq_scale_table[:].bitcast(I32), 0)
        nc.vector.memset(weight_scale_rows[:].bitcast(I32), 0)

        xa_rows = xa.rearrange("(p t) c -> p t c", t=PACK)
        xb_rows = xb.rearrange("(p t) c -> p t c", t=PACK)
        xa_planes = [keep.tile([P, T], F32, name="xa_plane%d" % t) for t in range(PACK)]
        xb_planes = [keep.tile([P, S], F32, name="xb_plane%d" % t) for t in range(PACK)]
        xq_table = keep.tile([P, S], U16, name="xq_table", align_bytes=64)
        factors = keep.tile([P, PACK], F32, name="factors")
        w_loaded = keep.tile([P, N], I32, name="w_loaded", align_bytes=64)
        wq_loaded = keep.tile([P, N], I32, name="wq_loaded", align_bytes=64)

        def load_plane(planes, rows, t):
            nc.sync.dma_start(out=planes[t][:], in_=rows[:, t, :])

        low, high = range(QUADRANTS // 2), range(QUADRANTS // 2, QUADRANTS)
        nc.sync.dma_start(list_b[:], offs2)
        nc.sync.dma_start(out=xq_table[:].bitcast(I32), in_=xq_words[0].bitcast(I32))
        nc.sync.dma_start(list_a[:], offs)
        load_plane(xa_planes, xa_rows, 0)
        load_plane(xa_planes, xa_rows, 1)
        load_scale_rows(nc, xq_scale_table, xq_scales, 0, low)
        nc.sync.dma_start(out=factors[:], in_=fk.rearrange("(p t) o -> p (t o)", t=PACK))
        load_plane(xb_planes, xb_rows, 0)
        load_scale_rows(nc, xq_scale_table, xq_scales, 0, high)
        load_plane(xa_planes, xa_rows, 2)
        load_scale_rows(nc, weight_scale_rows, wq_scales, 0, low)
        load_plane(xb_planes, xb_rows, 1)
        load_scale_rows(nc, weight_scale_rows, wq_scales, 0, high)
        load_plane(xb_planes, xb_rows, 2)
        load_scale_rows(nc, weight_scale_rows, w_scales, W_ROW, range(QUADRANTS))
        nc.sync.dma_start(out=wq_loaded[:], in_=wq_words[0].rearrange("p n t -> p (n t)").bitcast(I32))
        load_plane(xa_planes, xa_rows, 3)
        load_plane(xb_planes, xb_rows, 3)
        nc.sync.dma_start(out=w_loaded[:], in_=w_words[0].rearrange("p n t -> p (n t)").bitcast(I32))

        xq_picked = keep.tile([P, J], U16, name="xq_picked", align_bytes=64)
        nc.vector.tensor_copy(xq_picked[:], xq_table[:].indirect(list_b[:]))

        last = PACK - 1
        pr_grouped = keep.tile([P, J, PACK], BF16, name="pr_grouped", align_bytes=64)
        for t in range(last):
            xa_picked = keep.tile([P, J], F32, name="xa_picked%d" % t)
            products = keep.tile([P, J], F32, name="products%d" % t)
            nc.vector.tensor_copy(xa_picked[:], xa_planes[t][:].indirect(list_a[:]))
            nc.vector.tensor_tensor(products[:], xb_planes[t][:].indirect(list_b[:]), xa_picked[:], MULT)
            nc.scalar.activation(pr_grouped[:, :, t], products[:], COPY, scale=factors[:, t : t + 1])

        early_scales = keep.tile([P, EARLY * SLICE], U8, name="early_scales", align_bytes=64)
        nc.vector.tensor_copy(early_scales[:], xq_scale_table[:].indirect(list_b[:, : EARLY * LIST_COLS]))

        w_dealt = keep.tile([P, PACK, P], I32, name="w_dealt", align_bytes=64)
        wq_dealt = keep.tile([P, PACK, P], I32, name="wq_dealt", align_bytes=64)
        weight_scales = keep.tile([P, PACK, P], U8, name="weight_scales", align_bytes=64)
        deal_columns(nc, weight_scales, weight_scale_rows, LINE)
        deal_columns(nc, wq_dealt, wq_loaded, LINE // 4)
        deal_columns(nc, w_dealt, w_loaded, LINE // 4)

        run_ranges = [[(0, PACK)]] * (SLICES - 1) + [[(0, PACK // 2), (PACK // 2, PACK)]]
        banks = [
            [psum.tile([P, PACK, SLICE], F32, name="bank%d_%d" % (s, first)) for first, end in run_ranges[s]]
            for s in range(SLICES)
        ]

        def multiply_xq(s, picked_scales):
            cols = slice(s * SLICE, (s + 1) * SLICE)
            for bank, (first, end) in zip(banks[s], run_ranges[s]):
                for t in range(first, end):
                    nc.tensor.matmul_mx(
                        out=bank[:, t, :],
                        lhsT=wq_dealt[:, t, :].bitcast(FP8X4),
                        lhsT_scale=weight_scales[:, t, :],
                        rhs=xq_picked[:, cols].bitcast(FP4X4),
                        rhs_scale=picked_scales,
                        start=(t == first),
                        stop=False,
                    )

        for s in range(EARLY):
            multiply_xq(s, early_scales[:, s * SLICE : (s + 1) * SLICE])

        pr_scales = keep.tile([P, J], U8, name="pr_scales", align_bytes=64)
        y_codes = keep.tile([P, J], U32, name="y_codes", align_bytes=64)
        y_scales = keep.tile([P, J], U8, name="y_scales", align_bytes=64)
        y_rows = out_0.rearrange("(p t) j -> p t j", t=PACK)
        y_words = out_1[0].rearrange("p j t -> p (j t)").bitcast(I32)
        xa_slices = {}
        y_slices = {}

        def pick_xa(s):
            xa_slices[s] = keep.tile([P, SLICE], F32, name="xa_slice%d" % s, tag="xa_slice%d" % (s % 2), align_bytes=64)
            picks = list_a[:, s * LIST_COLS : (s + 1) * LIST_COLS]
            nc.vector.tensor_copy(xa_slices[s][:], xa_planes[last][:].indirect(picks))

        def finish_pr(s):
            cols = slice(s * SLICE, (s + 1) * SLICE)
            picks = list_b[:, s * LIST_COLS : (s + 1) * LIST_COLS]
            if s < SLICES - 1:
                product = keep.tile([P, SLICE], F32, name="product%d" % s, tag="product", bufs=2)
            else:
                product = keep.tile([P, SLICE], F32, name="product%d" % s, tag="pr_codes1", align_bytes=64)
            nc.vector.tensor_tensor(product[:], xb_planes[last][:].indirect(picks), xa_slices[s][:], MULT)
            nc.scalar.activation(pr_grouped[:, cols, last], product[:], COPY, scale=factors[:, last : last + 1])
            if s >= EARLY:
                late_scales = keep.tile(
                    [P, SLICE], U8, name="late_scales%d" % s, tag="xa_slice%d" % (s % 2), align_bytes=64
                )
                nc.vector.tensor_copy(late_scales[:], xq_scale_table[:].indirect(picks))
                multiply_xq(s, late_scales[:])

        def multiply_pr(s):
            cols = slice(s * SLICE, (s + 1) * SLICE)
            pr_codes = keep.tile([P, SLICE], U32, name="pr_codes%d" % s, align_bytes=64)
            nc.vector.quantize_mx(
                out=pr_codes[:].bitcast(FP8X4),
                scales=pr_scales[:, cols],
                in_=pr_grouped[:, cols, :].rearrange("p j t -> p (j t)"),
            )
            for bank, (first, end) in zip(banks[s], run_ranges[s]):
                for t in range(first, end):
                    nc.tensor.matmul_mx(
                        out=bank[:, t, :],
                        lhsT=w_dealt[:, t, :].bitcast(FP8X4),
                        lhsT_scale=weight_scales[W_ROW:P, t, :],
                        rhs=pr_codes[:].bitcast(FP8X4),
                        rhs_scale=pr_scales[:, cols],
                        start=False,
                        stop=(t == end - 1),
                    )

        def store_y(s):
            cols = slice(s * SLICE, (s + 1) * SLICE)
            y_slices[s] = keep.tile([P, PACK, SLICE], F32, name="y%d" % s)
            for bank, (first, end) in zip(banks[s], run_ranges[s]):
                nc.scalar.copy(y_slices[s][:, first:end, :], bank[:, first:end, :])
            nc.sync.dma_start(out=y_rows[:, :, cols], in_=y_slices[s][:])

        y_grouped = keep.tile([P, J, PACK], BF16, name="y_grouped", align_bytes=64)

        def round_y(first, end):
            s = first // SLICE
            nc.vector.tensor_copy(
                y_grouped[:, first:end, :].rearrange("p (c i) t -> p c t i", i=LINE // 4),
                y_slices[s][:, :, first - s * SLICE : end - s * SLICE].rearrange("p t (c i) -> p c t i", i=LINE // 4),
            )

        def quantize_y(first, end):
            nc.vector.quantize_mx(
                out=y_codes[:, first:end].bitcast(FP8X4),
                scales=y_scales[:, first:end],
                in_=y_grouped[:, first:end, :].rearrange("p j t -> p (j t)"),
            )

        stages = ((store_y, 3), (finish_pr, 1), (multiply_pr, 2), (pick_xa, 0))
        steps = SLICES + max(delay for stage, delay in stages)
        for step in range(steps):
            for stage, delay in stages:
                if 0 <= step - delay < SLICES:
                    stage(step - delay)
            if step == steps - 2:
                nc.scalar.copy(y_grouped[:, :SLICE, :], banks[0][0][:].rearrange("p t j -> p j t"))

        tail = J - SLICE
        round_y(SLICE, 2 * SLICE)
        round_y(2 * SLICE, tail)
        quantize_y(0, 2 * SLICE)
        quantize_y(2 * SLICE, tail)
        nc.sync.dma_start(out=y_words[:, :tail], in_=y_codes[:, :tail].bitcast(I32))
        halves = ((tail, tail + SLICE // 2), (tail + SLICE // 2, J))
        for first, end in halves:
            round_y(first, end)
        for first, end in halves:
            quantize_y(first, end)
        nc.sync.dma_start(out=y_words[:, tail:], in_=y_codes[:, tail:].bitcast(I32))

        for q in range(QUADRANTS):
            queue = nc.sync if q % 2 == 0 else nc.scalar
            queue.dma_start(
                out=out_2[0, SCALE_ROWS * q : SCALE_ROWS * (q + 1), :].bitcast(I32),
                in_=y_scales[QUADRANT * q : QUADRANT * q + SCALE_ROWS, :].bitcast(I32),
            )
